import numpy as np
import ml_dtypes


def mxq(x, axis, fmt="e4m3"):
    dtype, down = {"e4m3": (ml_dtypes.float8_e4m3fn, 7), "e5m2": (ml_dtypes.float8_e5m2, 14)}[fmt]
    v = np.moveaxis(np.asarray(x, np.float32).astype(ml_dtypes.bfloat16).astype(np.float64), axis, -1)
    blocks = v.reshape(v.shape[:-1] + (-1, 32))
    amax = np.abs(blocks).max(-1, keepdims=True)
    byte = np.maximum(np.where(amax > 0, np.frexp(amax)[1] - 1 + 127, 0) - down, 1)
    scale = np.exp2(byte - 127.0)
    codes = (blocks / scale).astype(np.float32).astype(dtype).astype(np.float64)
    return np.moveaxis((codes * scale).reshape(v.shape), -1, axis)


WIDE = False


def mx_kscale(k):
    if not WIDE:
        return np.ones(k)
    levels = np.array([30, -30])
    if k % 512:
        return np.exp2(np.random.permutation(np.resize(levels, k // 32))).repeat(32)
    a = np.empty((k // 512, 16))
    for p in range(k // 512):
        a[p, :8] = np.random.permutation(np.resize(levels, 8))
        for g in range(8):
            far = levels[np.abs(levels - a[p, g]) >= 10]
            a[p, g + 8] = far[np.random.randint(len(far))]
    return np.exp2(a.ravel()).repeat(32)


def f64(x):
    return np.asarray(x).astype(np.float64)


def striped(idx):
    return np.tile(np.asarray(idx).reshape(-1, 16).T, (8, 1)).astype(np.uint16)


def unstriped(offs):
    return offs[:16].T.reshape(-1).astype(np.int64)


E2M1 = np.array([0.0, 0.5, 1.0, 1.5, 2.0, 3.0, 4.0, 6.0, -0.0, -0.5, -1.0, -1.5, -2.0, -3.0, -4.0, -6.0])


def pack_weight(w, fmt):
    k, n = w.shape
    w = f64(np.asarray(w, np.float32).astype(ml_dtypes.bfloat16)).reshape(k // 32, 32, n)
    amax = np.abs(w).max(1)
    if fmt == "e4m3":
        byte = np.frexp(amax)[1] - 1 + 127 - 7
    else:
        mant, ex = np.frexp(amax / 6.0)
        byte = np.where(mant > 0.5, ex, ex - 1) + 127
    byte = np.clip(np.where(amax > 0, byte, 1), 1, 254)
    scaled = (w * np.exp2(127.0 - byte)[:, None, :]).reshape(k, n).astype(np.float32)
    by_word = np.ascontiguousarray(scaled.reshape(k // 512, 128, 4, n).transpose(0, 1, 3, 2))
    if fmt == "e4m3":
        words = by_word.astype(ml_dtypes.float8_e4m3fn).view(np.uint8)
    else:
        c = by_word.astype(ml_dtypes.float4_e2m1fn).view(np.uint8) & 0xF
        words = (c[..., 0::2] | (c[..., 1::2] << 4)).reshape(k // 512, 128, 2 * n)
    return np.ascontiguousarray(words), np.ascontiguousarray(byte.astype(np.uint8).reshape(k // 512, 16, n))


def unpack_weight(words, scales, fmt):
    g, _, n = scales.shape
    words = np.ascontiguousarray(words).reshape(g, 128, n, -1)
    if fmt == "e4m3":
        vals = words.view(ml_dtypes.float8_e4m3fn).astype(np.float64)
    else:
        nib = np.empty((g, 128, n, 4), np.uint8)
        nib[..., 0::2] = words & 0xF
        nib[..., 1::2] = words >> 4
        vals = E2M1[nib]
    vals = vals * np.repeat(np.exp2(scales.astype(np.float64) - 127.0), 8, axis=1)[..., None]
    return vals.transpose(0, 1, 3, 2).reshape(g * 512, n)


N, M, K, T, J = 1024, 512, 512, 1024, 512


def setup_inputs():
    n = np.random.standard_normal
    idx = np.random.permutation(T)[:J]
    idx2 = np.random.permutation(T)[:J]
    fn = mx_kscale(N)
    fm = mx_kscale(M)
    gp = pack_weight(n((N, J)) / fn[:, None], "e4m3")
    wup = pack_weight(n((N, M)) * 1 / np.sqrt(N) * fn[:, None] * fm, "e2m1")
    wlp = pack_weight(n((M, K)) * 1 / np.sqrt(M) / fm[:, None], "e4m3")
    return {
        "g_words": gp[0],
        "g_scales": gp[1],
        "wu_words": wup[0],
        "wu_scales": wup[1],
        "gt": (n((M, T)) * fm[:, None]).astype(np.float32),
        "wl_words": wlp[0],
        "wl_scales": wlp[1],
        "offs": striped(idx),
        "offs2": striped(idx2),
    }


def reference(g_words, g_scales, wu_words, wu_scales, gt, wl_words, wl_scales, offs, offs2):
    idx = unstriped(offs)
    idx2 = unstriped(offs2)
    gu = unpack_weight(g_words, g_scales, "e4m3")
    wuu = unpack_weight(wu_words, wu_scales, "e2m1")
    wlu = unpack_weight(wl_words, wl_scales, "e4m3")
    d = wuu.T @ gu
    pa = np.zeros((M, T))
    pa[:, idx] = d
    pb = np.zeros((M, T))
    pb[:, idx2] = d
    s = 0.5 * (pa + pb) + f64(gt)
    sq = mxq(s, 0, "e5m2")
    y = wlu.T @ sq
    return y

@@ -1,0 +1,172 @@
+from contextlib import ExitStack
+
+import concourse.mybir as mybir
+from concourse.masks import make_identity
+
+N, M, K, T, J = 1024, 512, 512, 1024, 512
+FLOPS = 2 * N * M * J + 2 * M * K * T
+
+F32 = mybir.dt.float32
+BF16 = mybir.dt.bfloat16
+I32 = mybir.dt.int32
+U32 = mybir.dt.uint32
+U16 = mybir.dt.uint16
+U8 = mybir.dt.uint8
+E4M3 = mybir.dt.float8_e4m3fn_x4
+E5M2 = mybir.dt.float8_e5m2_x4
+E2M1 = mybir.dt.float4_e2m1fn_x4
+MULT = mybir.AluOpType.mult
+COPY = mybir.ActivationFunctionType.Copy
+
+P = 128
+BANK = 512
+PASSES = N // 512
+SLICES = M // P
+PAIR = 2 * P
+PAIRS = T // PAIR
+HALVES = T // BANK
+
+
+def tile_list_merged_gradient_back_kernel(
+    tc, g_words, g_scales, wu_words, wu_scales, gt, wl_words, wl_scales, offs, offs2, out
+):
+    nc = tc.nc
+    with ExitStack() as ctx:
+        keep = ctx.enter_context(tc.tile_pool(name="keep", bufs=1))
+        psum = ctx.enter_context(tc.psum_pool(name="psum", bufs=1))
+
+        banks = [psum.tile([P, BANK], F32, name=f"bank{b}") for b in range(8)]
+
+        list_a = keep.tile([P, J // 16], U16, name="list_a")
+        list_b = keep.tile([P, J // 16], U16, name="list_b")
+        g_codes = keep.tile([P, PASSES, J], U32, name="g_codes", align_bytes=64)
+        wu_codes = keep.tile([P, PASSES, 2 * M], U8, name="wu_codes", align_bytes=64)
+        wl_codes = keep.tile([P, K], U32, name="wl_codes", align_bytes=64)
+        g_plane = keep.tile([P, PASSES, J], U8, name="g_plane", align_bytes=64)
+        wu_plane = keep.tile([P, PASSES, M], U8, name="wu_plane", align_bytes=64)
+        wl_plane = keep.tile([P, 1, K], U8, name="wl_plane", align_bytes=64)
+        page_a = keep.tile([P, T], F32, name="page_a")
+        page_b = keep.tile([P, T], F32, name="page_b")
+        ident = keep.tile([P, P], F32, name="ident")
+        own = [keep.tile([P, T], F32, name=f"own{r}") for r in range(SLICES)]
+        halved = [keep.tile([P, J], F32, name=f"halved{r}") for r in range(SLICES)]
+        lead = keep.tile([P, P], F32, name="lead")
+        turned = [keep.tile([P, 2, 2, P, 2], BF16, name=f"turned{c}") for c in range(PAIRS)]
+        woven = [keep.tile([P, PAIR * 4], BF16, name=f"woven{c}", align_bytes=64) for c in range(PAIRS)]
+        s_codes = [keep.tile([P, BANK], U32, name=f"s_codes{h}", align_bytes=64) for h in range(HALVES)]
+        s_plane = [keep.tile([P, BANK], U8, name=f"s_plane{h}", align_bytes=64) for h in range(HALVES)]
+        result = [keep.tile([P, BANK], F32, name=f"result{i}") for i in range(8)]
+
+        def load_scale_rows(queue, plane, scales, q):
+            queue.dma_start(
+                out=plane[32 * q : 32 * q + 4, :, :].bitcast(I32),
+                in_=scales[:, 4 * q : 4 * q + 4, :].rearrange("z r c -> r z c").bitcast(I32),
+            )
+
+        nc.vector.memset(page_a[:], 0.0)
+        nc.vector.memset(page_b[:], 0.0)
+        make_identity(nc, ident[:])
+
+        for q in range(2):
+            load_scale_rows(nc.scalar, wu_plane, wu_scales, q)
+            load_scale_rows(nc.sync, g_plane, g_scales, q)
+        nc.sync.dma_start(out=g_codes[:].bitcast(I32), in_=g_words.rearrange("z p c r -> p z (c r)").bitcast(I32))
+        nc.scalar.dma_start(out=wu_codes[:].bitcast(I32), in_=wu_words.rearrange("z p b -> p z b").bitcast(I32))
+        for q in range(2, 4):
+            load_scale_rows(nc.scalar, wu_plane, wu_scales, q)
+            load_scale_rows(nc.sync, g_plane, g_scales, q)
+        nc.sync.dma_start(out=list_a[:], in_=offs)
+        nc.sync.dma_start(out=list_b[:], in_=offs2)
+        for r in range(SLICES):
+            nc.sync.dma_start(out=own[r][:], in_=gt[r * P : (r + 1) * P, :])
+        nc.sync.dma_start(out=wl_codes[:].bitcast(I32), in_=wl_words[0].rearrange("p c r -> p (c r)").bitcast(I32))
+        for q in range(4):
+            load_scale_rows(nc.sync, wl_plane, wl_scales, q)
+
+        def first_product(r, bank, lo, hi):
+            for z in range(PASSES):
+                nc.tensor.matmul_mx(
+                    out=bank[:, lo:hi],
+                    lhsT=wu_codes[:, z, 2 * P * r : 2 * P * (r + 1)].bitcast(E2M1),
+                    lhsT_scale=wu_plane[:, z, P * r : P * (r + 1)],
+                    rhs=g_codes[:, z, lo:hi].bitcast(E4M3),
+                    rhs_scale=g_plane[:, z, lo:hi],
+                    start=(z == 0),
+                    stop=(z == PASSES - 1),
+                )
+
+        first_product(0, banks[7], 0, P)
+        nc.vector.tensor_scalar(out=lead[:], in0=banks[7][:, 0:P], scalar1=0.5, scalar2=None, op0=MULT)
+        for lo in range(P, J, P):
+            first_product(0, banks[0], lo, lo + P)
+        nc.scalar.activation(out=halved[0][:, P:J], in_=banks[0][:, P:J], func=COPY, scale=0.5)
+        for r in range(1, SLICES):
+            first_product(r, banks[r], 0, J)
+            nc.scalar.activation(out=halved[r][:], in_=banks[r][:], func=COPY, scale=0.5)
+
+        def add_turned(source, first, last):
+            for b in range(T // P):
+                c, i = divmod(b, 2)
+                nc.tensor.matmul(
+                    out=banks[4 + c][:, i * P : (i + 1) * P],
+                    lhsT=source[:, b * P : (b + 1) * P],
+                    rhs=ident[:],
+                    is_transpose=True,
+                    start=(first and i == 0),
+                    stop=(last and i == 1),
+                )
+
+        for r in range(SLICES):
+            if r == 0:
+                nc.vector.tensor_copy(out=page_a[:].indirect(list_a[:, 0:8]), in_=lead[:])
+                nc.vector.tensor_copy(out=page_b[:].indirect(list_b[:, 0:8]), in_=lead[:])
+                nc.vector.tensor_copy(out=page_a[:].indirect(list_a[:, 8:32]), in_=halved[0][:, P:J])
+                nc.vector.tensor_copy(out=page_b[:].indirect(list_b[:, 8:32]), in_=halved[0][:, P:J])
+                add_turned(page_a, True, False)
+                add_turned(own[r], False, False)
+            else:
+                nc.vector.tensor_copy(out=page_a[:].indirect(list_a[:]), in_=halved[r][:])
+                add_turned(page_a, True, False)
+                add_turned(own[r], False, False)
+                nc.vector.tensor_copy(out=page_b[:].indirect(list_b[:]), in_=halved[r][:])
+            add_turned(page_b, False, True)
+            for c in range(PAIRS):
+                src = banks[4 + c][:, 0:PAIR].rearrange("t (i q u e) -> t i u q e", i=2, u=2, e=2)
+                dst = turned[c][:, :, :, 32 * r : 32 * (r + 1), :]
+                if r == SLICES - 1 and c % 2 == 1:
+                    nc.vector.tensor_copy(out=dst, in_=src)
+                else:
+                    nc.scalar.copy(out=dst, in_=src)
+
+        for c in range(PAIRS):
+            words = turned[c][:].rearrange("t i u p e -> t (i u p e)").bitcast(F32)
+            for iu in range(4):
+                nc.tensor.transpose(banks[c][:, iu * P : (iu + 1) * P], words[:, iu * P : (iu + 1) * P], ident[:])
+            src = banks[c][:].rearrange("p (i u t) -> p i t u", i=2, u=2)
+            dst = woven[c][:].bitcast(F32).rearrange("p (i t u) -> p i t u", i=2, u=2)
+            if c == 1:
+                nc.vector.tensor_copy(out=dst, in_=src)
+            else:
+                nc.scalar.copy(out=dst, in_=src)
+            h, half_pair = divmod(c, 2)
+            cols = slice(half_pair * PAIR, (half_pair + 1) * PAIR)
+            nc.vector.quantize_mx(out=s_codes[h][:, cols].bitcast(E5M2), scales=s_plane[h][:, cols], in_=woven[c][:])
+
+        for h in range(HALVES):
+            for kt in range(K // P):
+                i = 4 * h + kt
+                bank = banks[(4 + i) % 8]
+                nc.tensor.matmul_mx(
+                    out=bank[:],
+                    lhsT=wl_codes[:, kt * P : (kt + 1) * P].bitcast(E4M3),
+                    lhsT_scale=wl_plane[:, 0, kt * P : (kt + 1) * P],
+                    rhs=s_codes[h][:].bitcast(E5M2),
+                    rhs_scale=s_plane[h][:],
+                    start=True,
+                    stop=True,
+                )
+                if i % 2 == 0:
+                    nc.scalar.copy(out=result[i][:], in_=bank[:])
+                else:
+                    nc.vector.tensor_copy(out=result[i][:], in_=bank[:])
+                nc.sync.dma_start(out=out[kt * P : (kt + 1) * P, h * BANK : (h + 1) * BANK], in_=result[i][:])

@@ -15,16 +15,17 @@ U8 = mybir.dt.uint8
 E4M3 = mybir.dt.float8_e4m3fn_x4
 E5M2 = mybir.dt.float8_e5m2_x4
 E2M1 = mybir.dt.float4_e2m1fn_x4
-MULT = mybir.AluOpType.mult
+ADD = mybir.AluOpType.add
 COPY = mybir.ActivationFunctionType.Copy
 
 P = 128
+PACK = 4
 BANK = 512
-PASSES = N // 512
-SLICES = M // P
-PAIR = 2 * P
-PAIRS = T // PAIR
+PASSES = N // (P * PACK)
+QUARTER = T // 4
 HALVES = T // BANK
+ENTRIES = 16
+ORDER = (0, 1, 3, 2)
 
 
 def tile_list_merged_gradient_back_kernel(
@@ -37,25 +38,28 @@ def tile_list_merged_gradient_back_kernel(
 
         banks = [psum.tile([P, BANK], F32, name=f"bank{b}") for b in range(8)]
 
-        list_a = keep.tile([P, J // 16], U16, name="list_a")
-        list_b = keep.tile([P, J // 16], U16, name="list_b")
+        list_a = keep.tile([P, J // ENTRIES], U16, name="list_a")
+        list_b = keep.tile([P, J // ENTRIES], U16, name="list_b")
         g_codes = keep.tile([P, PASSES, J], U32, name="g_codes", align_bytes=64)
-        wu_codes = keep.tile([P, PASSES, 2 * M], U8, name="wu_codes", align_bytes=64)
-        wl_codes = keep.tile([P, K], U32, name="wl_codes", align_bytes=64)
         g_plane = keep.tile([P, PASSES, J], U8, name="g_plane", align_bytes=64)
-        wu_plane = keep.tile([P, PASSES, M], U8, name="wu_plane", align_bytes=64)
+        wu_raw = keep.tile([P, PASSES, M], U16, name="wu_raw")
+        wu_raw_plane = keep.tile([P, PASSES, M], U8, name="wu_raw_plane")
+        wu_first = keep.tile([P, PASSES, 1, P], U16, name="wu_first", align_bytes=64)
+        wu_first_plane = keep.tile([P, PASSES, 1, P], U8, name="wu_first_plane", align_bytes=64)
+        wu_rest = keep.tile([P, PASSES, PACK - 1, P], U16, name="wu_rest", align_bytes=64)
+        wu_rest_plane = keep.tile([P, PASSES, PACK - 1, P], U8, name="wu_rest_plane", align_bytes=64)
+        wl_codes = keep.tile([P, K], U32, name="wl_codes", align_bytes=64)
         wl_plane = keep.tile([P, 1, K], U8, name="wl_plane", align_bytes=64)
         page_a = keep.tile([P, T], F32, name="page_a")
-        page_b = keep.tile([P, T], F32, name="page_b")
+        page_b = keep.tile([P, T + QUARTER], F32, name="page_b")
         ident = keep.tile([P, P], F32, name="ident")
-        own = [keep.tile([P, T], F32, name=f"own{r}") for r in range(SLICES)]
-        halved = [keep.tile([P, J], F32, name=f"halved{r}") for r in range(SLICES)]
-        lead = keep.tile([P, P], F32, name="lead")
-        turned = [keep.tile([P, 2, 2, P, 2], BF16, name=f"turned{c}") for c in range(PAIRS)]
-        woven = [keep.tile([P, PAIR * 4], BF16, name=f"woven{c}", align_bytes=64) for c in range(PAIRS)]
+        own = [keep.tile([P, T], F32, name=f"own{i}") for i in range(PACK)]
+        halved = [keep.tile([P, J], F32, name=f"halved{i}") for i in range(PACK)]
+        turned = [keep.tile([P, BANK], F32, name=f"turned{b}") for b in range(4)]
+        woven = [keep.tile([P, QUARTER * PACK], BF16, name=f"woven{c}", align_bytes=64) for c in range(4)]
         s_codes = [keep.tile([P, BANK], U32, name=f"s_codes{h}", align_bytes=64) for h in range(HALVES)]
         s_plane = [keep.tile([P, BANK], U8, name=f"s_plane{h}", align_bytes=64) for h in range(HALVES)]
-        result = [keep.tile([P, BANK], F32, name=f"result{i}") for i in range(8)]
+        result = [keep.tile([P, BANK], F32, name=f"result{n}") for n in range(8)]
 
         def load_scale_rows(queue, plane, scales, q):
             queue.dma_start(
@@ -63,101 +67,135 @@ def tile_list_merged_gradient_back_kernel(
                 in_=scales[:, 4 * q : 4 * q + 4, :].rearrange("z r c -> r z c").bitcast(I32),
             )
 
-        nc.vector.memset(page_a[:], 0.0)
-        nc.vector.memset(page_b[:], 0.0)
+        nc.gpsimd.memset(wu_raw_plane[:].bitcast(I32), 0)
+        nc.gpsimd.memset(page_a[:], 0.0)
+        nc.gpsimd.memset(page_b[:], 0.0)
         make_identity(nc, ident[:])
 
         for q in range(2):
-            load_scale_rows(nc.scalar, wu_plane, wu_scales, q)
             load_scale_rows(nc.sync, g_plane, g_scales, q)
+        for q in range(4):
+            load_scale_rows(nc.sync, wu_raw_plane, wu_scales, q)
+        nc.sync.dma_start(out=wu_raw[:].bitcast(I32), in_=wu_words.rearrange("z p b -> p z b").bitcast(I32))
         nc.sync.dma_start(out=g_codes[:].bitcast(I32), in_=g_words.rearrange("z p c r -> p z (c r)").bitcast(I32))
-        nc.scalar.dma_start(out=wu_codes[:].bitcast(I32), in_=wu_words.rearrange("z p b -> p z b").bitcast(I32))
         for q in range(2, 4):
-            load_scale_rows(nc.scalar, wu_plane, wu_scales, q)
             load_scale_rows(nc.sync, g_plane, g_scales, q)
         nc.sync.dma_start(out=list_a[:], in_=offs)
         nc.sync.dma_start(out=list_b[:], in_=offs2)
-        for r in range(SLICES):
-            nc.sync.dma_start(out=own[r][:], in_=gt[r * P : (r + 1) * P, :])
+        for i in ORDER:
+            nc.sync.dma_start(out=own[i][:], in_=gt.rearrange("(p i) t -> p i t", i=PACK)[:, i, :])
         nc.sync.dma_start(out=wl_codes[:].bitcast(I32), in_=wl_words[0].rearrange("p c r -> p (c r)").bitcast(I32))
         for q in range(4):
             load_scale_rows(nc.sync, wl_plane, wl_scales, q)
 
-        def first_product(r, bank, lo, hi):
+        def deal(engine, dealt, raw, lo, hi):
+            engine.tensor_copy(out=dealt[:], in_=raw[:].rearrange("p z (q i) -> p z i q", i=PACK)[:, :, lo:hi, :])
+
+        deal(nc.vector, wu_first_plane, wu_raw_plane, 0, 1)
+        deal(nc.vector, wu_first, wu_raw, 0, 1)
+        deal(nc.vector, wu_rest_plane, wu_raw_plane, 1, PACK)
+        deal(nc.vector, wu_rest, wu_raw, 1, PACK)
+
+        def first_product(i, bank, lo, hi):
+            codes, plane, slot = (wu_first, wu_first_plane, 0) if i == 0 else (wu_rest, wu_rest_plane, i - 1)
             for z in range(PASSES):
                 nc.tensor.matmul_mx(
                     out=bank[:, lo:hi],
-                    lhsT=wu_codes[:, z, 2 * P * r : 2 * P * (r + 1)].bitcast(E2M1),
-                    lhsT_scale=wu_plane[:, z, P * r : P * (r + 1)],
+                    lhsT=codes[:, z, slot, :].bitcast(E2M1),
+                    lhsT_scale=plane[:, z, slot, :],
                     rhs=g_codes[:, z, lo:hi].bitcast(E4M3),
                     rhs_scale=g_plane[:, z, lo:hi],
                     start=(z == 0),
                     stop=(z == PASSES - 1),
                 )
 
-        first_product(0, banks[7], 0, P)
-        nc.vector.tensor_scalar(out=lead[:], in0=banks[7][:, 0:P], scalar1=0.5, scalar2=None, op0=MULT)
-        for lo in range(P, J, P):
-            first_product(0, banks[0], lo, lo + P)
-        nc.scalar.activation(out=halved[0][:, P:J], in_=banks[0][:, P:J], func=COPY, scale=0.5)
-        for r in range(1, SLICES):
-            first_product(r, banks[r], 0, J)
-            nc.scalar.activation(out=halved[r][:], in_=banks[r][:], func=COPY, scale=0.5)
+        def halve(i, bank, lo, hi):
+            nc.scalar.activation(out=halved[i][:, lo:hi], in_=bank[:, lo:hi], func=COPY, scale=0.5)
 
-        def add_turned(source, first, last):
+        first_product(0, banks[2], 0, P)
+        halve(0, banks[2], 0, P)
+        first_product(0, banks[3], P, 2 * P)
+        halve(0, banks[3], P, 2 * P)
+        for lo in range(2 * P, J, P):
+            first_product(0, banks[4], lo, lo + P)
+        halve(0, banks[4], 2 * P, J)
+        for i in ORDER[1:]:
+            first_product(i, banks[4 + i], 0, J)
+            halve(i, banks[4 + i], 0, J)
+
+        def scatter(page, offsets, i, lo, hi):
+            nc.vector.tensor_copy(
+                out=page[:].indirect(offsets[:, lo // ENTRIES : hi // ENTRIES]), in_=halved[i][:, lo:hi]
+            )
+
+        def add_turned(pair, source, first, last):
             for b in range(T // P):
-                c, i = divmod(b, 2)
+                h, col = divmod(b * P, BANK)
                 nc.tensor.matmul(
-                    out=banks[4 + c][:, i * P : (i + 1) * P],
+                    out=banks[pair + h][:, col : col + P],
                     lhsT=source[:, b * P : (b + 1) * P],
                     rhs=ident[:],
                     is_transpose=True,
-                    start=(first and i == 0),
-                    stop=(last and i == 1),
+                    start=(first and col == 0),
+                    stop=(last and col == BANK - P),
                 )
 
-        for r in range(SLICES):
-            if r == 0:
-                nc.vector.tensor_copy(out=page_a[:].indirect(list_a[:, 0:8]), in_=lead[:])
-                nc.vector.tensor_copy(out=page_b[:].indirect(list_b[:, 0:8]), in_=lead[:])
-                nc.vector.tensor_copy(out=page_a[:].indirect(list_a[:, 8:32]), in_=halved[0][:, P:J])
-                nc.vector.tensor_copy(out=page_b[:].indirect(list_b[:, 8:32]), in_=halved[0][:, P:J])
-                add_turned(page_a, True, False)
-                add_turned(own[r], False, False)
-            else:
-                nc.vector.tensor_copy(out=page_a[:].indirect(list_a[:]), in_=halved[r][:])
-                add_turned(page_a, True, False)
-                add_turned(own[r], False, False)
-                nc.vector.tensor_copy(out=page_b[:].indirect(list_b[:]), in_=halved[r][:])
-            add_turned(page_b, False, True)
-            for c in range(PAIRS):
-                src = banks[4 + c][:, 0:PAIR].rearrange("t (i q u e) -> t i u q e", i=2, u=2, e=2)
-                dst = turned[c][:, :, :, 32 * r : 32 * (r + 1), :]
-                if r == SLICES - 1 and c % 2 == 1:
-                    nc.vector.tensor_copy(out=dst, in_=src)
-                else:
-                    nc.scalar.copy(out=dst, in_=src)
+        def turn_back(pair, i):
+            for h in range(HALVES):
+                nc.scalar.copy(out=turned[pair + h][:], in_=banks[pair + h][:])
+            for b in range(T // P):
+                h, col = divmod(b * P, BANK)
+                c, at = divmod(b * P, QUARTER)
+                at = at + (i % 2) * QUARTER
+                nc.tensor.transpose(banks[4 + c][:, at : at + P], turned[pair + h][:, col : col + P], ident[:])
 
-        for c in range(PAIRS):
-            words = turned[c][:].rearrange("t i u p e -> t (i u p e)").bitcast(F32)
-            for iu in range(4):
-                nc.tensor.transpose(banks[c][:, iu * P : (iu + 1) * P], words[:, iu * P : (iu + 1) * P], ident[:])
-            src = banks[c][:].rearrange("p (i u t) -> p i t u", i=2, u=2)
-            dst = woven[c][:].bitcast(F32).rearrange("p (i t u) -> p i t u", i=2, u=2)
-            if c == 1:
-                nc.vector.tensor_copy(out=dst, in_=src)
+        def two_rows(c):
+            return banks[4 + c][:].rearrange("p (e t) -> p t e", e=2)
+
+        def words(c):
+            return woven[c][:].rearrange("p (t i) -> p t i", i=PACK)
+
+        for step, i in enumerate(ORDER):
+            pair = 2 * (step % 2)
+            last = step == PACK - 1
+            if step == 0:
+                scatter(page_a, list_a, i, 0, P)
+                scatter(page_b, list_b, i, 0, 2 * P)
+                scatter(page_a, list_a, i, P, J)
+                scatter(page_b, list_b, i, 2 * P, J)
             else:
-                nc.scalar.copy(out=dst, in_=src)
-            h, half_pair = divmod(c, 2)
-            cols = slice(half_pair * PAIR, (half_pair + 1) * PAIR)
-            nc.vector.quantize_mx(out=s_codes[h][:, cols].bitcast(E5M2), scales=s_plane[h][:, cols], in_=woven[c][:])
+                scatter(page_a, list_a, i, 0, J)
+            add_turned(pair, page_a, not last, last)
+            if not last:
+                add_turned(pair, own[i], False, False)
+            if step == PACK - 2:
+                add_turned(2 - pair, own[ORDER[-1]], True, False)
+            if step > 0:
+                scatter(page_b, list_b, i, 0, J)
+            if not last:
+                add_turned(pair, page_b, False, True)
+            turn_back(pair, i)
+            if step == 1:
+                for c in range(4):
+                    nc.scalar.copy(out=words(c)[:, :, 0:2], in_=two_rows(c))
+
+        for h in range(HALVES):
+            for c in (2 * h, 2 * h + 1):
+                placed = page_b[:].rearrange("p (c t) -> p c t", t=QUARTER)[:, c :: 4 - c, :]
+                nc.vector.tensor_tensor(
+                    out=words(c)[:, :, 2:4], in0=placed.rearrange("p e t -> p t e"), in1=two_rows(c), op=ADD
+                )
+            for c in (2 * h, 2 * h + 1):
+                cols = slice((c % 2) * QUARTER, (c % 2 + 1) * QUARTER)
+                nc.vector.quantize_mx(
+                    out=s_codes[h][:, cols].bitcast(E5M2), scales=s_plane[h][:, cols], in_=woven[c][:]
+                )
 
         for h in range(HALVES):
             for kt in range(K // P):
-                i = 4 * h + kt
-                bank = banks[(4 + i) % 8]
+                n = 4 * h + kt
                 nc.tensor.matmul_mx(
-                    out=bank[:],
+                    out=banks[n][:],
                     lhsT=wl_codes[:, kt * P : (kt + 1) * P].bitcast(E4M3),
                     lhsT_scale=wl_plane[:, 0, kt * P : (kt + 1) * P],
                     rhs=s_codes[h][:].bitcast(E5M2),
@@ -165,8 +203,13 @@ def tile_list_merged_gradient_back_kernel(
                     start=True,
                     stop=True,
                 )
-                if i % 2 == 0:
-                    nc.scalar.copy(out=result[i][:], in_=bank[:])
-                else:
-                    nc.vector.tensor_copy(out=result[i][:], in_=bank[:])
-                nc.sync.dma_start(out=out[kt * P : (kt + 1) * P, h * BANK : (h + 1) * BANK], in_=result[i][:])
+                width = BANK // 2 if n == 0 else BANK
+                for lo in range(0, BANK, width):
+                    cols = slice(lo, lo + width)
+                    if n in (4, 6):
+                        nc.vector.tensor_copy(out=result[n][:, cols], in_=banks[n][:, cols])
+                    else:
+                        nc.scalar.copy(out=result[n][:, cols], in_=banks[n][:, cols])
+                    nc.sync.dma_start(
+                        out=out[kt * P : (kt + 1) * P, h * BANK + lo : h * BANK + lo + width], in_=result[n][:, cols]
+                    )

@@ -67,21 +67,23 @@ def tile_list_merged_gradient_back_kernel(
                 in_=scales[:, 4 * q : 4 * q + 4, :].rearrange("z r c -> r z c").bitcast(I32),
             )
 
-        nc.gpsimd.memset(wu_raw_plane[:].bitcast(I32), 0)
-        nc.gpsimd.memset(page_a[:], 0.0)
-        nc.gpsimd.memset(page_b[:], 0.0)
+        nc.vector.memset(wu_raw_plane[:].bitcast(I32), 0)
+        nc.vector.memset(page_a[:], 0.0)
+        nc.vector.memset(page_b[:], 0.0)
         make_identity(nc, ident[:])
 
+        g_view = g_words.rearrange("z p c r -> p z (c r)").bitcast(I32)
         for q in range(2):
             load_scale_rows(nc.sync, g_plane, g_scales, q)
+        nc.sync.dma_start(out=wu_raw[:].bitcast(I32), in_=wu_words.rearrange("z p b -> p z b").bitcast(I32))
         for q in range(4):
             load_scale_rows(nc.sync, wu_raw_plane, wu_scales, q)
-        nc.sync.dma_start(out=wu_raw[:].bitcast(I32), in_=wu_words.rearrange("z p b -> p z b").bitcast(I32))
-        nc.sync.dma_start(out=g_codes[:].bitcast(I32), in_=g_words.rearrange("z p c r -> p z (c r)").bitcast(I32))
+        nc.sync.dma_start(out=g_codes[:, :, 0 : J // 2].bitcast(I32), in_=g_view[:, :, 0 : J // 2])
         for q in range(2, 4):
             load_scale_rows(nc.sync, g_plane, g_scales, q)
         nc.sync.dma_start(out=list_a[:], in_=offs)
         nc.sync.dma_start(out=list_b[:], in_=offs2)
+        nc.sync.dma_start(out=g_codes[:, :, J // 2 : J].bitcast(I32), in_=g_view[:, :, J // 2 : J])
         for i in ORDER:
             nc.sync.dma_start(out=own[i][:], in_=gt.rearrange("(p i) t -> p i t", i=PACK)[:, i, :])
         nc.sync.dma_start(out=wl_codes[:].bitcast(I32), in_=wl_words[0].rearrange("p c r -> p (c r)").bitcast(I32))

@@ -20,10 +20,12 @@ COPY = mybir.ActivationFunctionType.Copy
 
 P = 128
 PACK = 4
+QUADRANTS = 4
 BANK = 512
 PASSES = N // (P * PACK)
-QUARTER = T // 4
 HALVES = T // BANK
+QUARTERS = 4
+QUARTER = T // QUARTERS
 ENTRIES = 16
 ORDER = (0, 1, 3, 2)
 
@@ -41,72 +43,69 @@ def tile_list_merged_gradient_back_kernel(
         list_a = keep.tile([P, J // ENTRIES], U16, name="list_a")
         list_b = keep.tile([P, J // ENTRIES], U16, name="list_b")
         g_codes = keep.tile([P, PASSES, J], U32, name="g_codes", align_bytes=64)
-        g_plane = keep.tile([P, PASSES, J], U8, name="g_plane", align_bytes=64)
+        g_scale = keep.tile([P, PASSES, J], U8, name="g_scale", align_bytes=64)
         wu_raw = keep.tile([P, PASSES, M], U16, name="wu_raw")
-        wu_raw_plane = keep.tile([P, PASSES, M], U8, name="wu_raw_plane")
+        wu_raw_scale = keep.tile([P, PASSES, M], U8, name="wu_raw_scale")
         wu_first = keep.tile([P, PASSES, 1, P], U16, name="wu_first", align_bytes=64)
-        wu_first_plane = keep.tile([P, PASSES, 1, P], U8, name="wu_first_plane", align_bytes=64)
+        wu_first_scale = keep.tile([P, PASSES, 1, P], U8, name="wu_first_scale", align_bytes=64)
         wu_rest = keep.tile([P, PASSES, PACK - 1, P], U16, name="wu_rest", align_bytes=64)
-        wu_rest_plane = keep.tile([P, PASSES, PACK - 1, P], U8, name="wu_rest_plane", align_bytes=64)
+        wu_rest_scale = keep.tile([P, PASSES, PACK - 1, P], U8, name="wu_rest_scale", align_bytes=64)
         wl_codes = keep.tile([P, K], U32, name="wl_codes", align_bytes=64)
-        wl_plane = keep.tile([P, 1, K], U8, name="wl_plane", align_bytes=64)
+        wl_scale = keep.tile([P, 1, K], U8, name="wl_scale", align_bytes=64)
         page_a = keep.tile([P, T], F32, name="page_a")
         page_b = keep.tile([P, T + QUARTER], F32, name="page_b")
         ident = keep.tile([P, P], F32, name="ident")
         own = [keep.tile([P, T], F32, name=f"own{i}") for i in range(PACK)]
         halved = [keep.tile([P, J], F32, name=f"halved{i}") for i in range(PACK)]
-        turned = [keep.tile([P, BANK], F32, name=f"turned{b}") for b in range(4)]
-        woven = [keep.tile([P, QUARTER * PACK], BF16, name=f"woven{c}", align_bytes=64) for c in range(4)]
+        turned = [keep.tile([P, BANK], F32, name=f"turned{b}") for b in range(2 * HALVES)]
+        woven = [keep.tile([P, QUARTER * PACK], BF16, name=f"woven{c}", align_bytes=64) for c in range(QUARTERS)]
         s_codes = [keep.tile([P, BANK], U32, name=f"s_codes{h}", align_bytes=64) for h in range(HALVES)]
-        s_plane = [keep.tile([P, BANK], U8, name=f"s_plane{h}", align_bytes=64) for h in range(HALVES)]
-        result = [keep.tile([P, BANK], F32, name=f"result{n}") for n in range(8)]
+        s_scale = [keep.tile([P, BANK], U8, name=f"s_scale{h}", align_bytes=64) for h in range(HALVES)]
+        result = [keep.tile([P, BANK], F32, name=f"result{n}") for n in range(HALVES * K // P)]
 
-        def load_scale_rows(queue, plane, scales, q):
-            queue.dma_start(
-                out=plane[32 * q : 32 * q + 4, :, :].bitcast(I32),
-                in_=scales[:, 4 * q : 4 * q + 4, :].rearrange("z r c -> r z c").bitcast(I32),
-            )
-
-        nc.vector.memset(wu_raw_plane[:].bitcast(I32), 0)
+        nc.vector.memset(wu_raw_scale[:].bitcast(I32), 0)
         nc.vector.memset(page_a[:], 0.0)
         nc.vector.memset(page_b[:], 0.0)
         make_identity(nc, ident[:])
 
+        def load_scale_rows(scale, scales, quadrants):
+            for q in quadrants:
+                nc.sync.dma_start(
+                    out=scale[32 * q : 32 * q + 4, :, :].bitcast(I32),
+                    in_=scales[:, 4 * q : 4 * q + 4, :].rearrange("z r c -> r z c").bitcast(I32),
+                )
+
         g_view = g_words.rearrange("z p c r -> p z (c r)").bitcast(I32)
-        for q in range(2):
-            load_scale_rows(nc.sync, g_plane, g_scales, q)
+        load_scale_rows(g_scale, g_scales, range(QUADRANTS // 2))
         nc.sync.dma_start(out=wu_raw[:].bitcast(I32), in_=wu_words.rearrange("z p b -> p z b").bitcast(I32))
-        for q in range(4):
-            load_scale_rows(nc.sync, wu_raw_plane, wu_scales, q)
+        load_scale_rows(wu_raw_scale, wu_scales, range(QUADRANTS))
         nc.sync.dma_start(out=g_codes[:, :, 0 : J // 2].bitcast(I32), in_=g_view[:, :, 0 : J // 2])
-        for q in range(2, 4):
-            load_scale_rows(nc.sync, g_plane, g_scales, q)
+        load_scale_rows(g_scale, g_scales, range(QUADRANTS // 2, QUADRANTS))
         nc.sync.dma_start(out=list_a[:], in_=offs)
         nc.sync.dma_start(out=list_b[:], in_=offs2)
         nc.sync.dma_start(out=g_codes[:, :, J // 2 : J].bitcast(I32), in_=g_view[:, :, J // 2 : J])
         for i in ORDER:
             nc.sync.dma_start(out=own[i][:], in_=gt.rearrange("(p i) t -> p i t", i=PACK)[:, i, :])
         nc.sync.dma_start(out=wl_codes[:].bitcast(I32), in_=wl_words[0].rearrange("p c r -> p (c r)").bitcast(I32))
-        for q in range(4):
-            load_scale_rows(nc.sync, wl_plane, wl_scales, q)
+        load_scale_rows(wl_scale, wl_scales, range(QUADRANTS))
 
-        def deal(engine, dealt, raw, lo, hi):
-            engine.tensor_copy(out=dealt[:], in_=raw[:].rearrange("p z (q i) -> p z i q", i=PACK)[:, :, lo:hi, :])
+        def deal(dealt, raw, lo, hi):
+            nc.vector.tensor_copy(out=dealt[:], in_=raw[:].rearrange("p z (q i) -> p z i q", i=PACK)[:, :, lo:hi, :])
 
-        deal(nc.vector, wu_first_plane, wu_raw_plane, 0, 1)
-        deal(nc.vector, wu_first, wu_raw, 0, 1)
-        deal(nc.vector, wu_rest_plane, wu_raw_plane, 1, PACK)
-        deal(nc.vector, wu_rest, wu_raw, 1, PACK)
+        deal(wu_first_scale, wu_raw_scale, 0, 1)
+        deal(wu_first, wu_raw, 0, 1)
+        deal(wu_rest_scale, wu_raw_scale, 1, PACK)
+        deal(wu_rest, wu_raw, 1, PACK)
 
         def first_product(i, bank, lo, hi):
-            codes, plane, slot = (wu_first, wu_first_plane, 0) if i == 0 else (wu_rest, wu_rest_plane, i - 1)
+            codes, scale, at = (wu_first, wu_first_scale, 0) if i == 0 else (wu_rest, wu_rest_scale, i - 1)
             for z in range(PASSES):
                 nc.tensor.matmul_mx(
                     out=bank[:, lo:hi],
-                    lhsT=codes[:, z, slot, :].bitcast(E2M1),
-                    lhsT_scale=plane[:, z, slot, :],
+                    lhsT=codes[:, z, at, :].bitcast(E2M1),
+                    lhsT_scale=scale[:, z, at, :],
                     rhs=g_codes[:, z, lo:hi].bitcast(E4M3),
-                    rhs_scale=g_plane[:, z, lo:hi],
+                    rhs_scale=g_scale[:, z, lo:hi],
                     start=(z == 0),
                     stop=(z == PASSES - 1),
                 )
@@ -114,13 +113,10 @@ def tile_list_merged_gradient_back_kernel(
         def halve(i, bank, lo, hi):
             nc.scalar.activation(out=halved[i][:, lo:hi], in_=bank[:, lo:hi], func=COPY, scale=0.5)
 
-        first_product(0, banks[2], 0, P)
-        halve(0, banks[2], 0, P)
-        first_product(0, banks[3], P, 2 * P)
-        halve(0, banks[3], P, 2 * P)
-        for lo in range(2 * P, J, P):
-            first_product(0, banks[4], lo, lo + P)
-        halve(0, banks[4], 2 * P, J)
+        for bank, lo, hi in ((banks[2], 0, P), (banks[3], P, 2 * P), (banks[4], 2 * P, J)):
+            for col in range(lo, hi, P):
+                first_product(0, bank, col, col + P)
+            halve(0, bank, lo, hi)
         for i in ORDER[1:]:
             first_product(i, banks[4 + i], 0, J)
             halve(i, banks[4 + i], 0, J)
@@ -130,7 +126,7 @@ def tile_list_merged_gradient_back_kernel(
                 out=page[:].indirect(offsets[:, lo // ENTRIES : hi // ENTRIES]), in_=halved[i][:, lo:hi]
             )
 
-        def add_turned(pair, source, first, last):
+        def add_transposed(pair, source, first, last):
             for b in range(T // P):
                 h, col = divmod(b * P, BANK)
                 nc.tensor.matmul(
@@ -151,12 +147,13 @@ def tile_list_merged_gradient_back_kernel(
                 at = at + (i % 2) * QUARTER
                 nc.tensor.transpose(banks[4 + c][:, at : at + P], turned[pair + h][:, col : col + P], ident[:])
 
-        def two_rows(c):
+        def two_sets(c):
             return banks[4 + c][:].rearrange("p (e t) -> p t e", e=2)
 
-        def words(c):
+        def four_sets(c):
             return woven[c][:].rearrange("p (t i) -> p t i", i=PACK)
 
+        add_transposed(0, own[ORDER[0]], True, False)
         for step, i in enumerate(ORDER):
             pair = 2 * (step % 2)
             last = step == PACK - 1
@@ -167,48 +164,46 @@ def tile_list_merged_gradient_back_kernel(
                 scatter(page_b, list_b, i, 2 * P, J)
             else:
                 scatter(page_a, list_a, i, 0, J)
-            add_turned(pair, page_a, not last, last)
+            add_transposed(pair, page_a, False, last)
             if not last:
-                add_turned(pair, own[i], False, False)
-            if step == PACK - 2:
-                add_turned(2 - pair, own[ORDER[-1]], True, False)
+                add_transposed(2 - pair, own[ORDER[step + 1]], True, False)
             if step > 0:
                 scatter(page_b, list_b, i, 0, J)
             if not last:
-                add_turned(pair, page_b, False, True)
+                add_transposed(pair, page_b, False, True)
             turn_back(pair, i)
-            if step == 1:
-                for c in range(4):
-                    nc.scalar.copy(out=words(c)[:, :, 0:2], in_=two_rows(c))
+            if i == 1:
+                for c in range(QUARTERS):
+                    nc.scalar.copy(out=four_sets(c)[:, :, 0:2], in_=two_sets(c))
 
         for h in range(HALVES):
             for c in (2 * h, 2 * h + 1):
-                placed = page_b[:].rearrange("p (c t) -> p c t", t=QUARTER)[:, c :: 4 - c, :]
+                placed = page_b[:].rearrange("p (c t) -> p c t", t=QUARTER)[:, c :: QUARTERS - c, :]
                 nc.vector.tensor_tensor(
-                    out=words(c)[:, :, 2:4], in0=placed.rearrange("p e t -> p t e"), in1=two_rows(c), op=ADD
+                    out=four_sets(c)[:, :, 2:4], in0=placed.rearrange("p e t -> p t e"), in1=two_sets(c), op=ADD
                 )
             for c in (2 * h, 2 * h + 1):
                 cols = slice((c % 2) * QUARTER, (c % 2 + 1) * QUARTER)
                 nc.vector.quantize_mx(
-                    out=s_codes[h][:, cols].bitcast(E5M2), scales=s_plane[h][:, cols], in_=woven[c][:]
+                    out=s_codes[h][:, cols].bitcast(E5M2), scales=s_scale[h][:, cols], in_=woven[c][:]
                 )
 
         for h in range(HALVES):
             for kt in range(K // P):
-                n = 4 * h + kt
+                n = h * (K // P) + kt
                 nc.tensor.matmul_mx(
                     out=banks[n][:],
                     lhsT=wl_codes[:, kt * P : (kt + 1) * P].bitcast(E4M3),
-                    lhsT_scale=wl_plane[:, 0, kt * P : (kt + 1) * P],
+                    lhsT_scale=wl_scale[:, 0, kt * P : (kt + 1) * P],
                     rhs=s_codes[h][:].bitcast(E5M2),
-                    rhs_scale=s_plane[h][:],
+                    rhs_scale=s_scale[h][:],
                     start=True,
                     stop=True,
                 )
                 width = BANK // 2 if n == 0 else BANK
                 for lo in range(0, BANK, width):
                     cols = slice(lo, lo + width)
-                    if n in (4, 6):
+                    if h == 1 and kt % 2 == 0:
                         nc.vector.tensor_copy(out=result[n][:, cols], in_=banks[n][:, cols])
                     else:
                         nc.scalar.copy(out=result[n][:, cols], in_=banks[n][:, cols])

from contextlib import ExitStack

import concourse.mybir as mybir
from concourse.masks import make_identity

N, M, K, T, J = 1024, 512, 512, 1024, 512
FLOPS = 2 * N * M * J + 2 * M * K * T

F32 = mybir.dt.float32
BF16 = mybir.dt.bfloat16
I32 = mybir.dt.int32
U32 = mybir.dt.uint32
U16 = mybir.dt.uint16
U8 = mybir.dt.uint8
E4M3 = mybir.dt.float8_e4m3fn_x4
E5M2 = mybir.dt.float8_e5m2_x4
E2M1 = mybir.dt.float4_e2m1fn_x4
ADD = mybir.AluOpType.add
COPY = mybir.ActivationFunctionType.Copy

P = 128
PACK = 4
QUADRANTS = 4
BANK = 512
PASSES = N // (P * PACK)
HALVES = T // BANK
QUARTERS = 4
QUARTER = T // QUARTERS
ENTRIES = 16
ORDER = (0, 1, 3, 2)


def tile_list_merged_gradient_back_kernel(
    tc, g_words, g_scales, wu_words, wu_scales, gt, wl_words, wl_scales, offs, offs2, out
):
    nc = tc.nc
    with ExitStack() as ctx:
        keep = ctx.enter_context(tc.tile_pool(name="keep", bufs=1))
        psum = ctx.enter_context(tc.psum_pool(name="psum", bufs=1))

        banks = [psum.tile([P, BANK], F32, name=f"bank{b}") for b in range(8)]

        list_a = keep.tile([P, J // ENTRIES], U16, name="list_a")
        list_b = keep.tile([P, J // ENTRIES], U16, name="list_b")
        g_codes = keep.tile([P, PASSES, J], U32, name="g_codes", align_bytes=64)
        g_scale = keep.tile([P, PASSES, J], U8, name="g_scale", align_bytes=64)
        wu_raw = keep.tile([P, PASSES, M], U16, name="wu_raw")
        wu_raw_scale = keep.tile([P, PASSES, M], U8, name="wu_raw_scale")
        wu_first = keep.tile([P, PASSES, 1, P], U16, name="wu_first", align_bytes=64)
        wu_first_scale = keep.tile([P, PASSES, 1, P], U8, name="wu_first_scale", align_bytes=64)
        wu_rest = keep.tile([P, PASSES, PACK - 1, P], U16, name="wu_rest", align_bytes=64)
        wu_rest_scale = keep.tile([P, PASSES, PACK - 1, P], U8, name="wu_rest_scale", align_bytes=64)
        wl_codes = keep.tile([P, K], U32, name="wl_codes", align_bytes=64)
        wl_scale = keep.tile([P, 1, K], U8, name="wl_scale", align_bytes=64)
        page_a = keep.tile([P, T], F32, name="page_a")
        page_b = keep.tile([P, T + QUARTER], F32, name="page_b")
        ident = keep.tile([P, P], F32, name="ident")
        own = [keep.tile([P, T], F32, name=f"own{i}") for i in range(PACK)]
        halved = [keep.tile([P, J], F32, name=f"halved{i}") for i in range(PACK)]
        turned = [keep.tile([P, BANK], F32, name=f"turned{b}") for b in range(2 * HALVES)]
        woven = [keep.tile([P, QUARTER * PACK], BF16, name=f"woven{c}", align_bytes=64) for c in range(QUARTERS)]
        s_codes = [keep.tile([P, BANK], U32, name=f"s_codes{h}", align_bytes=64) for h in range(HALVES)]
        s_scale = [keep.tile([P, BANK], U8, name=f"s_scale{h}", align_bytes=64) for h in range(HALVES)]
        result = [keep.tile([P, BANK], F32, name=f"result{n}") for n in range(HALVES * K // P)]

        nc.vector.memset(wu_raw_scale[:].bitcast(I32), 0)
        nc.vector.memset(page_a[:], 0.0)
        nc.vector.memset(page_b[:], 0.0)
        make_identity(nc, ident[:])

        def load_scale_rows(scale, scales, quadrants):
            for q in quadrants:
                nc.sync.dma_start(
                    out=scale[32 * q : 32 * q + 4, :, :].bitcast(I32),
                    in_=scales[:, 4 * q : 4 * q + 4, :].rearrange("z r c -> r z c").bitcast(I32),
                )

        g_view = g_words.rearrange("z p c r -> p z (c r)").bitcast(I32)
        load_scale_rows(g_scale, g_scales, range(QUADRANTS // 2))
        nc.sync.dma_start(out=wu_raw[:].bitcast(I32), in_=wu_words.rearrange("z p b -> p z b").bitcast(I32))
        load_scale_rows(wu_raw_scale, wu_scales, range(QUADRANTS))
        nc.sync.dma_start(out=g_codes[:, :, 0 : J // 2].bitcast(I32), in_=g_view[:, :, 0 : J // 2])
        load_scale_rows(g_scale, g_scales, range(QUADRANTS // 2, QUADRANTS))
        nc.sync.dma_start(out=list_a[:], in_=offs)
        nc.sync.dma_start(out=list_b[:], in_=offs2)
        nc.sync.dma_start(out=g_codes[:, :, J // 2 : J].bitcast(I32), in_=g_view[:, :, J // 2 : J])
        for i in ORDER:
            nc.sync.dma_start(out=own[i][:], in_=gt.rearrange("(p i) t -> p i t", i=PACK)[:, i, :])
        nc.sync.dma_start(out=wl_codes[:].bitcast(I32), in_=wl_words[0].rearrange("p c r -> p (c r)").bitcast(I32))
        load_scale_rows(wl_scale, wl_scales, range(QUADRANTS))

        def deal(dealt, raw, lo, hi):
            nc.vector.tensor_copy(out=dealt[:], in_=raw[:].rearrange("p z (q i) -> p z i q", i=PACK)[:, :, lo:hi, :])

        deal(wu_first_scale, wu_raw_scale, 0, 1)
        deal(wu_first, wu_raw, 0, 1)
        deal(wu_rest_scale, wu_raw_scale, 1, PACK)
        deal(wu_rest, wu_raw, 1, PACK)

        def first_product(i, bank, lo, hi):
            codes, scale, at = (wu_first, wu_first_scale, 0) if i == 0 else (wu_rest, wu_rest_scale, i - 1)
            for z in range(PASSES):
                nc.tensor.matmul_mx(
                    out=bank[:, lo:hi],
                    lhsT=codes[:, z, at, :].bitcast(E2M1),
                    lhsT_scale=scale[:, z, at, :],
                    rhs=g_codes[:, z, lo:hi].bitcast(E4M3),
                    rhs_scale=g_scale[:, z, lo:hi],
                    start=(z == 0),
                    stop=(z == PASSES - 1),
                )

        def halve(i, bank, lo, hi):
            nc.scalar.activation(out=halved[i][:, lo:hi], in_=bank[:, lo:hi], func=COPY, scale=0.5)

        for bank, lo, hi in ((banks[2], 0, P), (banks[3], P, 2 * P), (banks[4], 2 * P, J)):
            for col in range(lo, hi, P):
                first_product(0, bank, col, col + P)
            halve(0, bank, lo, hi)
        for i in ORDER[1:]:
            first_product(i, banks[4 + i], 0, J)
            halve(i, banks[4 + i], 0, J)

        def scatter(page, offsets, i, lo, hi):
            nc.vector.tensor_copy(
                out=page[:].indirect(offsets[:, lo // ENTRIES : hi // ENTRIES]), in_=halved[i][:, lo:hi]
            )

        def add_transposed(pair, source, first, last):
            for b in range(T // P):
                h, col = divmod(b * P, BANK)
                nc.tensor.matmul(
                    out=banks[pair + h][:, col : col + P],
                    lhsT=source[:, b * P : (b + 1) * P],
                    rhs=ident[:],
                    is_transpose=True,
                    start=(first and col == 0),
                    stop=(last and col == BANK - P),
                )

        def turn_back(pair, i):
            for h in range(HALVES):
                nc.scalar.copy(out=turned[pair + h][:], in_=banks[pair + h][:])
            for b in range(T // P):
                h, col = divmod(b * P, BANK)
                c, at = divmod(b * P, QUARTER)
                at = at + (i % 2) * QUARTER
                nc.tensor.transpose(banks[4 + c][:, at : at + P], turned[pair + h][:, col : col + P], ident[:])

        def two_sets(c):
            return banks[4 + c][:].rearrange("p (e t) -> p t e", e=2)

        def four_sets(c):
            return woven[c][:].rearrange("p (t i) -> p t i", i=PACK)

        add_transposed(0, own[ORDER[0]], True, False)
        for step, i in enumerate(ORDER):
            pair = 2 * (step % 2)
            last = step == PACK - 1
            if step == 0:
                scatter(page_a, list_a, i, 0, P)
                scatter(page_b, list_b, i, 0, 2 * P)
                scatter(page_a, list_a, i, P, J)
                scatter(page_b, list_b, i, 2 * P, J)
            else:
                scatter(page_a, list_a, i, 0, J)
            add_transposed(pair, page_a, False, last)
            if not last:
                add_transposed(2 - pair, own[ORDER[step + 1]], True, False)
            if step > 0:
                scatter(page_b, list_b, i, 0, J)
            if not last:
                add_transposed(pair, page_b, False, True)
            turn_back(pair, i)
            if i == 1:
                for c in range(QUARTERS):
                    nc.scalar.copy(out=four_sets(c)[:, :, 0:2], in_=two_sets(c))

        for h in range(HALVES):
            for c in (2 * h, 2 * h + 1):
                placed = page_b[:].rearrange("p (c t) -> p c t", t=QUARTER)[:, c :: QUARTERS - c, :]
                nc.vector.tensor_tensor(
                    out=four_sets(c)[:, :, 2:4], in0=placed.rearrange("p e t -> p t e"), in1=two_sets(c), op=ADD
                )
            for c in (2 * h, 2 * h + 1):
                cols = slice((c % 2) * QUARTER, (c % 2 + 1) * QUARTER)
                nc.vector.quantize_mx(
                    out=s_codes[h][:, cols].bitcast(E5M2), scales=s_scale[h][:, cols], in_=woven[c][:]
                )

        for h in range(HALVES):
            for kt in range(K // P):
                n = h * (K // P) + kt
                nc.tensor.matmul_mx(
                    out=banks[n][:],
                    lhsT=wl_codes[:, kt * P : (kt + 1) * P].bitcast(E4M3),
                    lhsT_scale=wl_scale[:, 0, kt * P : (kt + 1) * P],
                    rhs=s_codes[h][:].bitcast(E5M2),
                    rhs_scale=s_scale[h][:],
                    start=True,
                    stop=True,
                )
                width = BANK // 2 if n == 0 else BANK
                for lo in range(0, BANK, width):
                    cols = slice(lo, lo + width)
                    if h == 1 and kt % 2 == 0:
                        nc.vector.tensor_copy(out=result[n][:, cols], in_=banks[n][:, cols])
                    else:
                        nc.scalar.copy(out=result[n][:, cols], in_=banks[n][:, cols])
                    nc.sync.dma_start(
                        out=out[kt * P : (kt + 1) * P, h * BANK + lo : h * BANK + lo + width], in_=result[n][:, cols]
                    )
